import numpy as np
import ml_dtypes

BF16 = ml_dtypes.bfloat16


def bf(x):
    return np.asarray(x, np.float32).astype(BF16)


def f32(x):
    return np.asarray(x, np.float32)


def f64(x):
    return np.asarray(x).astype(np.float64)


def striped(idx):
    return np.tile(idx.reshape(-1, 16).T, (8, 1))


S, K, M, N, D, V = 1024, 128, 128, 512, 4, 128


def setup_inputs():
    return {"table": bf(np.random.standard_normal((K, S))), "w": bf(np.random.standard_normal((D, K, M)) / np.sqrt(D * K)), "b": f32(0.5 * np.random.standard_normal((M, 1))), "offs": striped(np.random.permutation(S)[:N])}


def reference(table, w, b, offs):
    idx = offs[:16].T.reshape(-1)
    x = f64(table)[:, idx]
    y = sum(f64(w)[t].T @ x[:, t * V : (t + 1) * V] for t in range(D))
    return np.tanh(y + f64(b))

@@ -1,0 +1,42 @@
+import concourse.mybir as mybir
+
+BF16, F32, U16 = mybir.dt.bfloat16, mybir.dt.float32, mybir.dt.uint16
+
+P = 128
+TABLE_NODES = 1024
+RELATIONS = 4
+NODES = 128
+PIECE_COLUMNS = NODES // 16
+
+FLOPS = 2 * P * P * RELATIONS * NODES
+
+
+def tile_gather_matmul_kernel(tc, table, w, b, offs, out):
+    nc = tc.nc
+    with (
+        tc.tile_pool(name="held", bufs=1) as held,
+        tc.psum_pool(name="psum", bufs=1) as psum,
+    ):
+        offsets = held.tile([P, RELATIONS * PIECE_COLUMNS], U16, name="offsets")
+        nc.sync.dma_start(offsets[:], offs)
+        nodes = held.tile([P, TABLE_NODES], BF16, name="nodes")
+        nc.scalar.dma_start(nodes[:], table)
+        weights = held.tile([P, RELATIONS, P], BF16, name="weights")
+        nc.sync.dma_start(weights[:], w.rearrange("t k m -> k t m"))
+        bias = held.tile([P, 1], F32, name="bias")
+        nc.gpsimd.dma_start(bias[:], b)
+
+        y = psum.tile([P, NODES], F32, name="y")
+        for t in range(RELATIONS):
+            piece = offsets[:, t * PIECE_COLUMNS : (t + 1) * PIECE_COLUMNS]
+            nc.tensor.matmul(
+                y[:],
+                weights[:, t, :],
+                nodes[:].indirect(piece),
+                start=(t == 0),
+                stop=(t == RELATIONS - 1),
+            )
+
+        result = held.tile([P, NODES], F32, name="result")
+        nc.scalar.activation(result[:], y[:], mybir.ActivationFunctionType.Tanh, bias=bias[:])
+        nc.sync.dma_start(out, result[:])

@@ -21,17 +21,23 @@ def tile_gather_matmul_kernel(tc, table, w, b, offs, out):
         nc.sync.dma_start(offsets[:], offs)
         nodes = held.tile([P, TABLE_NODES], BF16, name="nodes")
         nc.scalar.dma_start(nodes[:], table)
-        weights = held.tile([P, RELATIONS, P], BF16, name="weights")
-        nc.sync.dma_start(weights[:], w.rearrange("t k m -> k t m"))
+        weights = [held.tile([P, P], BF16, name=f"weights{t}") for t in range(RELATIONS)]
+        nc.sync.dma_start(weights[0][:], w[0])
         bias = held.tile([P, 1], F32, name="bias")
-        nc.gpsimd.dma_start(bias[:], b)
+        nc.sync.dma_start(bias[:], b)
+        for t in range(1, RELATIONS):
+            nc.scalar.dma_start(weights[t][:], w[t])
+
+        early = held.tile([P, 1], F32, name="early")
+        nc.vector.memset(early[:], 0.0)
+        nc.scalar.activation(early[:], early[:], mybir.ActivationFunctionType.Tanh)
 
         y = psum.tile([P, NODES], F32, name="y")
         for t in range(RELATIONS):
             piece = offsets[:, t * PIECE_COLUMNS : (t + 1) * PIECE_COLUMNS]
             nc.tensor.matmul(
                 y[:],
-                weights[:, t, :],
+                weights[t][:],
                 nodes[:].indirect(piece),
                 start=(t == 0),
                 stop=(t == RELATIONS - 1),

@@ -20,13 +20,13 @@ def tile_gather_matmul_kernel(tc, table, w, b, offs, out):
         offsets = held.tile([P, RELATIONS * PIECE_COLUMNS], U16, name="offsets")
         nc.sync.dma_start(offsets[:], offs)
         nodes = held.tile([P, TABLE_NODES], BF16, name="nodes")
-        nc.scalar.dma_start(nodes[:], table)
+        nc.sync.dma_start(nodes[:], table)
         weights = [held.tile([P, P], BF16, name=f"weights{t}") for t in range(RELATIONS)]
-        nc.sync.dma_start(weights[0][:], w[0])
+        nc.scalar.dma_start(weights[0][:], w[0])
         bias = held.tile([P, 1], F32, name="bias")
-        nc.sync.dma_start(bias[:], b)
+        nc.scalar.dma_start(bias[:], b)
         for t in range(1, RELATIONS):
-            nc.scalar.dma_start(weights[t][:], w[t])
+            nc.sync.dma_start(weights[t][:], w[t])
 
         early = held.tile([P, 1], F32, name="early")
         nc.vector.memset(early[:], 0.0)

@@ -7,6 +7,8 @@ TABLE_NODES = 1024
 RELATIONS = 4
 NODES = 128
 PIECE_COLUMNS = NODES // 16
+WARM_COLUMNS = 512
+WARM_MATMULS = 3
 
 FLOPS = 2 * P * P * RELATIONS * NODES
 
@@ -27,6 +29,12 @@ def tile_gather_matmul_kernel(tc, table, w, b, offs, out):
         nc.scalar.dma_start(bias[:], b)
         for t in range(1, RELATIONS):
             nc.sync.dma_start(weights[t][:], w[t])
+
+        zeros = held.tile([P, WARM_COLUMNS], BF16, name="zeros")
+        nc.vector.memset(zeros[:], 0.0)
+        unread = psum.tile([P, WARM_COLUMNS], F32, name="unread")
+        for turn in range(WARM_MATMULS):
+            nc.tensor.matmul(unread[:], zeros[:, 0:P], zeros[:], start=True, stop=True)
 
         early = held.tile([P, 1], F32, name="early")
         nc.vector.memset(early[:], 0.0)

@@ -23,12 +23,11 @@ def tile_gather_matmul_kernel(tc, table, w, b, offs, out):
         nc.sync.dma_start(offsets[:], offs)
         nodes = held.tile([P, TABLE_NODES], BF16, name="nodes")
         nc.sync.dma_start(nodes[:], table)
-        weights = [held.tile([P, P], BF16, name=f"weights{t}") for t in range(RELATIONS)]
-        nc.scalar.dma_start(weights[0][:], w[0])
+        pairs = [held.tile([P, 2, P], BF16, name=f"pair{h}") for h in range(RELATIONS // 2)]
+        nc.scalar.dma_start(pairs[0][:], w[0:2].rearrange("t k m -> k t m"))
         bias = held.tile([P, 1], F32, name="bias")
         nc.scalar.dma_start(bias[:], b)
-        for t in range(1, RELATIONS):
-            nc.sync.dma_start(weights[t][:], w[t])
+        nc.sync.dma_start(pairs[1][:], w[2:4].rearrange("t k m -> k t m"))
 
         zeros = held.tile([P, WARM_COLUMNS], BF16, name="zeros")
         nc.vector.memset(zeros[:], 0.0)
@@ -45,7 +44,7 @@ def tile_gather_matmul_kernel(tc, table, w, b, offs, out):
             piece = offsets[:, t * PIECE_COLUMNS : (t + 1) * PIECE_COLUMNS]
             nc.tensor.matmul(
                 y[:],
-                weights[t][:],
+                pairs[t // 2][:, t % 2, :],
                 nodes[:].indirect(piece),
                 start=(t == 0),
                 stop=(t == RELATIONS - 1),

@@ -24,10 +24,10 @@ def tile_gather_matmul_kernel(tc, table, w, b, offs, out):
         nodes = held.tile([P, TABLE_NODES], BF16, name="nodes")
         nc.sync.dma_start(nodes[:], table)
         pairs = [held.tile([P, 2, P], BF16, name=f"pair{h}") for h in range(RELATIONS // 2)]
-        nc.scalar.dma_start(pairs[0][:], w[0:2].rearrange("t k m -> k t m"))
+        for h in range(RELATIONS // 2):
+            nc.scalar.dma_start(pairs[h][:], w[2 * h : 2 * h + 2].rearrange("t k m -> k t m"))
         bias = held.tile([P, 1], F32, name="bias")
-        nc.scalar.dma_start(bias[:], b)
-        nc.sync.dma_start(pairs[1][:], w[2:4].rearrange("t k m -> k t m"))
+        nc.sync.dma_start(bias[:], b)
 
         zeros = held.tile([P, WARM_COLUMNS], BF16, name="zeros")
         nc.vector.memset(zeros[:], 0.0)

import concourse.mybir as mybir

BF16, F32, U16 = mybir.dt.bfloat16, mybir.dt.float32, mybir.dt.uint16

P = 128
TABLE_NODES = 1024
RELATIONS = 4
NODES = 128
PIECE_COLUMNS = NODES // 16
WARM_COLUMNS = 512
WARM_MATMULS = 3

FLOPS = 2 * P * P * RELATIONS * NODES


def tile_gather_matmul_kernel(tc, table, w, b, offs, out):
    nc = tc.nc
    with (
        tc.tile_pool(name="held", bufs=1) as held,
        tc.psum_pool(name="psum", bufs=1) as psum,
    ):
        offsets = held.tile([P, RELATIONS * PIECE_COLUMNS], U16, name="offsets")
        nc.sync.dma_start(offsets[:], offs)
        nodes = held.tile([P, TABLE_NODES], BF16, name="nodes")
        nc.sync.dma_start(nodes[:], table)
        pairs = [held.tile([P, 2, P], BF16, name=f"pair{h}") for h in range(RELATIONS // 2)]
        for h in range(RELATIONS // 2):
            nc.scalar.dma_start(pairs[h][:], w[2 * h : 2 * h + 2].rearrange("t k m -> k t m"))
        bias = held.tile([P, 1], F32, name="bias")
        nc.sync.dma_start(bias[:], b)

        zeros = held.tile([P, WARM_COLUMNS], BF16, name="zeros")
        nc.vector.memset(zeros[:], 0.0)
        unread = psum.tile([P, WARM_COLUMNS], F32, name="unread")
        for turn in range(WARM_MATMULS):
            nc.tensor.matmul(unread[:], zeros[:, 0:P], zeros[:], start=True, stop=True)

        early = held.tile([P, 1], F32, name="early")
        nc.vector.memset(early[:], 0.0)
        nc.scalar.activation(early[:], early[:], mybir.ActivationFunctionType.Tanh)

        y = psum.tile([P, NODES], F32, name="y")
        for t in range(RELATIONS):
            piece = offsets[:, t * PIECE_COLUMNS : (t + 1) * PIECE_COLUMNS]
            nc.tensor.matmul(
                y[:],
                pairs[t // 2][:, t % 2, :],
                nodes[:].indirect(piece),
                start=(t == 0),
                stop=(t == RELATIONS - 1),
            )

        result = held.tile([P, NODES], F32, name="result")
        nc.scalar.activation(result[:], y[:], mybir.ActivationFunctionType.Tanh, bias=bias[:])
        nc.sync.dma_start(out, result[:])
